import numpy as np
import ml_dtypes


def mxq(x, axis, fmt="e4m3"):
    dtype, down = {"e4m3": (ml_dtypes.float8_e4m3fn, 7), "e5m2": (ml_dtypes.float8_e5m2, 14)}[fmt]
    v = np.moveaxis(np.asarray(x, np.float32).astype(ml_dtypes.bfloat16).astype(np.float64), axis, -1)
    blocks = v.reshape(v.shape[:-1] + (-1, 32))
    amax = np.abs(blocks).max(-1, keepdims=True)
    byte = np.maximum(np.where(amax > 0, np.frexp(amax)[1] - 1 + 127, 0) - down, 1)
    scale = np.exp2(byte - 127.0)
    codes = (blocks / scale).astype(np.float32).astype(dtype).astype(np.float64)
    return np.moveaxis((codes * scale).reshape(v.shape), -1, axis)


WIDE = False


def mx_kscale(k):
    if not WIDE:
        return np.ones(k)
    levels = np.array([10, -10, 5, -5, 0])
    if k % 512:
        return np.exp2(np.random.permutation(np.resize(levels, k // 32))).repeat(32)
    a = np.empty((k // 512, 16))
    for p in range(k // 512):
        a[p, :8] = np.random.permutation(np.resize(levels, 8))
        for g in range(8):
            far = levels[np.abs(levels - a[p, g]) >= 10]
            a[p, g + 8] = far[np.random.randint(len(far))]
    return np.exp2(a.ravel()).repeat(32)


def f64(x):
    return np.asarray(x).astype(np.float64)


def striped(idx):
    return np.tile(idx.reshape(-1, 16).T, (8, 1)).astype(np.uint16)


def unstriped(offs):
    return offs[:16].T.reshape(-1).astype(np.int64)


def pack_weight(w):
    k, n = w.shape
    w = f64(np.asarray(w, np.float32).astype(ml_dtypes.bfloat16)).reshape(k // 32, 32, n)
    amax = np.abs(w).max(1)
    byte = np.clip(np.where(amax > 0, np.frexp(amax)[1] - 1 + 127 - 7, 1), 1, 254)
    scaled = (w * np.exp2(127.0 - byte)[:, None, :]).reshape(k, n).astype(np.float32)
    words = np.ascontiguousarray(scaled.reshape(k // 512, 128, 4, n).transpose(0, 1, 3, 2)).astype(ml_dtypes.float8_e4m3fn).view(np.uint8)
    return words, np.ascontiguousarray(byte.astype(np.uint8).reshape(k // 512, 16, n))


def unpack_weight(words, scales):
    g, p, n, _ = words.shape
    vals = np.ascontiguousarray(words).view(ml_dtypes.float8_e4m3fn).astype(np.float64) * np.repeat(np.exp2(scales.astype(np.float64) - 127.0), 8, axis=1)[..., None]
    return vals.transpose(0, 1, 3, 2).reshape(g * 512, n)


def planes(y):
    n, m = y.shape
    v = y.astype(np.float32).astype(ml_dtypes.bfloat16).astype(np.float64).reshape(n // 32, 32, m)
    top = np.abs(v).max(1)
    byte = np.clip(np.where(top > 0, np.frexp(top)[1] - 1 + 127 - 7, 1), 1, 254)
    codes = (v * np.exp2(127.0 - byte)[:, None, :]).reshape(n, m).astype(np.float32).astype(ml_dtypes.float8_e4m3fn).view(np.uint8)
    words = codes.reshape(n // 512, 128, 4, m).transpose(0, 1, 3, 2)
    return np.ascontiguousarray(words), np.ascontiguousarray(byte.astype(np.uint8).reshape(n // 512, 16, m))


K, T, S, N, H, W, U = 512, 2048, 512, 512, 512, 1024, 1024


def setup_inputs():
    n = np.random.standard_normal
    s = mx_kscale(K)[:, None]
    u = mx_kscale(H)
    packed_xT = pack_weight(n((K, T)) * s)
    packed_eT = pack_weight(n((K, W)) * s)
    return {
        "x_words": packed_xT[0],
        "x_scales": packed_xT[1],
        "w1": (n((K, N)) / np.sqrt(K) / s).astype(np.float32),
        "e_words": packed_eT[0],
        "e_scales": packed_eT[1],
        "w2": (n((K, N)) / np.sqrt(K) / s).astype(np.float32),
        "unit": (np.random.uniform(0.6, 1.4, (H, 1)) * u[:, None]).astype(np.float32),
        "w3": (n((H, N)) / np.sqrt(H) / u[:, None]).astype(np.float32),
        "offs": striped(np.random.permutation(T)[:S]),
        "ldr": striped(np.random.permutation(W)[:S]),
        "bo": striped(np.random.permutation(np.concatenate([np.arange(S), np.random.randint(0, S, U - S)]))),
        "ln": striped(np.random.permutation(np.concatenate([np.arange(S), np.random.randint(0, S, U - S)]))),
        "gu": striped(np.random.permutation(np.concatenate([np.arange(S), np.random.randint(0, S, U - S)]))),
    }


def reference(x_words, x_scales, w1, e_words, e_scales, w2, unit, w3, offs, ldr, bo, ln, gu):
    xq = unpack_weight(x_words, x_scales)[:, unstriped(offs)]
    y = mxq(f64(w1), 0, "e4m3").T @ xq
    yb2 = y[:, unstriped(bo)]
    e_ldr = unpack_weight(e_words, e_scales)[:, unstriped(ldr)]
    ye = mxq(f64(w2), 0, "e4m3").T @ e_ldr
    el = ye[:, unstriped(ln)]
    mt = np.maximum(yb2, el)
    yg2 = y[:, unstriped(gu)]
    hid = f64(unit) * (mt * yg2)
    out_0 = mxq(f64(w3), 0, "e4m3").T @ mxq(hid, 0, "e4m3")
    return (out_0,) + planes(out_0)

@@ -1,0 +1,211 @@
+from contextlib import ExitStack
+
+import concourse.mybir as mybir
+
+K, T, S, N, H, W, U = 512, 2048, 512, 512, 512, 1024, 1024
+FLOPS = 2 * K * N * S * 2 + 2 * H * N * U
+
+F32 = mybir.dt.float32
+BF16 = mybir.dt.bfloat16
+I32 = mybir.dt.int32
+U32 = mybir.dt.uint32
+U16 = mybir.dt.uint16
+U8 = mybir.dt.uint8
+FP8X4 = mybir.dt.float8_e4m3fn_x4
+MULT = mybir.AluOpType.mult
+MAX = mybir.AluOpType.max
+COPY = mybir.ActivationFunctionType.Copy
+
+P = 128
+PACK = 4
+HALF = N // 2
+CHUNKS = (256, 256, 256, 128, 128)
+LANES = 16
+RUN = 4
+
+
+def tile_picked_yborrow_max_po_kernel(
+    tc, x_words, x_scales, w1, e_words, e_scales, w2, unit, w3, offs, ldr, bo, ln, gu, out_0, out_1, out_2
+):
+    nc = tc.nc
+    with ExitStack() as ctx:
+        keep = ctx.enter_context(tc.tile_pool(name="keep", bufs=1))
+        ring = ctx.enter_context(tc.tile_pool(name="ring", bufs=2))
+        psum = ctx.enter_context(tc.psum_pool(name="psum", bufs=8))
+
+        def load_list(src, name):
+            tile = keep.tile(list(src.shape), U16, name=name)
+            nc.sync.dma_start(tile[:], src)
+            return tile
+
+        def load_scales(src, name, clear):
+            tile = keep.tile([P, src.shape[2]], U8, name=name, align_bytes=64)
+            clear.memset(tile[:].bitcast(I32), 0)
+            for q in range(4):
+                nc.sync.dma_start(tile[32 * q : 32 * q + 4, :].bitcast(I32), src[0, 4 * q : 4 * q + 4, :].bitcast(I32))
+            return tile
+
+        def load_words(src, name):
+            tile = keep.tile([P, src.shape[2]], I32, name=name, align_bytes=64)
+            nc.sync.dma_start(tile[:], src[0].rearrange("p n t -> p (n t)").bitcast(I32))
+            return tile
+
+        def load_weight(src, name):
+            rows = src.rearrange("(p j) c -> p j c", j=PACK)
+            halves = []
+            for h in range(2):
+                tile = keep.tile([P, PACK, HALF], F32, name=f"{name}_raw{h}")
+                nc.sync.dma_start(tile[:], rows[:, :, h * HALF : (h + 1) * HALF])
+                halves.append(tile)
+            return halves
+
+        def pick(table, offsets, dtype, name):
+            picked = keep.tile([P, S], dtype, name=name, align_bytes=64)
+            nc.vector.tensor_copy(picked[:], table[:].bitcast(dtype).indirect(offsets[:]))
+            return picked
+
+        def on_vector(out, in_):
+            nc.vector.tensor_copy(out, in_)
+
+        def on_scalar(out, in_):
+            nc.scalar.activation(out, in_, COPY)
+
+        def quantise_weight(halves, casts, name, codes_tag):
+            rounded = keep.tile([P, PACK, P, PACK], BF16, name=f"{name}_bf", tag="weight_rounded", align_bytes=64)
+            for h in range(2):
+                cols = slice(h * P // 2, (h + 1) * P // 2)
+                casts[h](
+                    rounded[:, :, cols, :].rearrange("p t m j -> p m j t"),
+                    halves[h][:].rearrange("p j (m t) -> p m j t", t=PACK),
+                )
+            codes = keep.tile([P, N], U32, name=f"{name}_codes", tag=codes_tag, align_bytes=64)
+            scales = keep.tile([P, N], U8, name=f"{name}_scales", align_bytes=64)
+            for t in range(PACK):
+                cols = slice(t * P, (t + 1) * P)
+                nc.vector.quantize_mx(
+                    codes[:, cols].bitcast(FP8X4), scales[:, cols], rounded[:, t].rearrange("p m j -> p (m j)")
+                )
+            return codes, scales
+
+        def product(out, weight, t, codes, scales):
+            cols = slice(t * P, (t + 1) * P)
+            nc.tensor.matmul_mx(
+                out,
+                lhsT=weight[0][:, cols].bitcast(FP8X4),
+                lhsT_scale=weight[1][:, cols],
+                rhs=codes.bitcast(FP8X4),
+                rhs_scale=scales,
+                start=True,
+                stop=True,
+            )
+
+        def first_layer(weight, codes, scales, name):
+            rows = []
+            for t in range(PACK):
+                bank = psum.tile([P, S], F32, name="bank")
+                product(bank[:], weight, t, codes[:], scales[:])
+                row = keep.tile([P, S], F32, name=f"{name}{t}")
+                nc.scalar.copy(row[:], bank[:])
+                rows.append(row)
+            return rows
+
+        ldr_sb = load_list(ldr, "ldr_sb")
+        offs_sb = load_list(offs, "offs_sb")
+        ln_sb = load_list(ln, "ln_sb")
+        bo_sb = load_list(bo, "bo_sb")
+        gu_sb = load_list(gu, "gu_sb")
+        unit_sb = keep.tile([P, PACK], F32, name="unit_sb")
+        nc.sync.dma_start(unit_sb[:], unit.rearrange("(p t) o -> p (t o)", t=PACK))
+        e_word_table = load_words(e_words, "e_word_table")
+        e_scale_table = load_scales(e_scales, "e_scale_table", nc.vector)
+        w2_raw = load_weight(w2, "w2")
+        w1_raw = load_weight(w1, "w1")
+        x_scale_table = load_scales(x_scales, "x_scale_table", nc.gpsimd)
+        x_word_table = load_words(x_words, "x_word_table")
+        w3_raw = load_weight(w3, "w3")
+
+        starts = [sum(CHUNKS[:c]) for c in range(len(CHUNKS))]
+
+        def look_up(move, rows, offsets, c, tile):
+            entries = slice(starts[c] // LANES, (starts[c] + CHUNKS[c]) // LANES)
+            for t in range(PACK):
+                move(tile[:, t, :], rows[t][:].indirect(offsets[:, entries]))
+            return tile
+
+        def lender_tile(c):
+            return keep.tile([P, PACK, CHUNKS[c]], F32, name=f"lender{c}", tag=f"lender_slot{c % 2}", align_bytes=64)
+
+        e_picked_words = pick(e_word_table, ldr_sb, U32, "e_picked_words")
+        e_picked_scales = pick(e_scale_table, ldr_sb, U8, "e_picked_scales")
+        w2_mx = quantise_weight(w2_raw, (on_scalar, on_vector), "w2", "w2_codes")
+        ye = first_layer(w2_mx, e_picked_words, e_picked_scales, "ye")
+        first_lender = look_up(on_scalar, ye, ln_sb, 0, lender_tile(0))
+
+        w1_mx = quantise_weight(w1_raw, (on_vector, on_vector), "w1", "lender_slot1")
+        x_picked_scales = pick(x_scale_table, offs_sb, U8, "x_picked_scales")
+        x_picked_words = pick(x_word_table, offs_sb, U32, "x_picked_words")
+        y = first_layer(w1_mx, x_picked_words, x_picked_scales, "y")
+        w3_mx = quantise_weight(w3_raw, (on_vector, on_vector), "w3", "w3_codes")
+
+        y_unit = []
+        for t in range(PACK):
+            row = keep.tile([P, S], F32, name=f"y_unit{t}")
+            nc.vector.tensor_scalar(row[:], y[t][:], unit_sb[:, t : t + 1], None, MULT)
+            y_unit.append(row)
+
+        out_rows = out_0.rearrange("(p t) r -> p t r", t=PACK)
+        out_words = out_1[0].rearrange("p c t -> p (c t)").bitcast(I32)
+        out_scales = keep.tile([P, U], U8, name="out_scales", align_bytes=64)
+
+        def interleaved(tile):
+            return tile[:].rearrange("p (c i) t -> p c t i", i=RUN)
+
+        def by_runs(tile):
+            return tile[:].rearrange("p t (c i) -> p c t i", i=RUN)
+
+        def risks(c):
+            width = CHUNKS[c]
+            borrower = look_up(on_scalar, y, bo_sb, c, ring.tile([P, PACK, width], F32, name="borrower"))
+            lender = first_lender if c == 0 else look_up(on_scalar, ye, ln_sb, c, lender_tile(c))
+            move = on_scalar if c == len(CHUNKS) - 1 else on_vector
+            guarantor = look_up(move, y_unit, gu_sb, c, ring.tile([P, PACK, width], F32, name="guarantor"))
+            larger = ring.tile([P, PACK, width], F32, name="larger")
+            nc.vector.tensor_tensor(larger[:], borrower[:], lender[:], MAX)
+            hid = keep.tile([P, width, PACK], BF16, name=f"hid{c}", tag="rounded_slot", align_bytes=64)
+            nc.vector.tensor_tensor(interleaved(hid), by_runs(larger), by_runs(guarantor), MULT)
+            hid_codes = keep.tile([P, width], U32, name=f"hid_codes{c}", tag=f"lender_slot{c % 2}", align_bytes=64)
+            hid_scales = ring.tile([P, width], U8, name="hid_scales", align_bytes=64)
+            nc.vector.quantize_mx(hid_codes[:].bitcast(FP8X4), hid_scales[:], hid[:].rearrange("p r t -> p (r t)"))
+            risk = ring.tile([P, PACK, width], F32, name="risk", bufs=3)
+            per_bank = S // width
+            for t0 in range(0, PACK, per_bank):
+                bank = psum.tile([P, per_bank, width], F32, name="bank")
+                for u in range(per_bank):
+                    product(bank[:, u, :], w3_mx, t0 + u, hid_codes[:], hid_scales[:])
+                nc.scalar.copy(risk[:, t0 : t0 + per_bank, :], bank[:])
+            nc.sync.dma_start(out_rows[:, :, starts[c] : starts[c] + width], risk[:])
+            return risk
+
+        def planes(c, risk):
+            width = CHUNKS[c]
+            loans = slice(starts[c], starts[c] + width)
+            risk_bf = keep.tile([P, width, PACK], BF16, name=f"risk_bf{c}", tag="rounded_slot", align_bytes=64)
+            nc.vector.tensor_copy(interleaved(risk_bf), by_runs(risk))
+            risk_codes = ring.tile([P, width], I32, name="risk_codes", align_bytes=64)
+            nc.vector.quantize_mx(
+                risk_codes[:].bitcast(FP8X4), out_scales[:, loans], risk_bf[:].rearrange("p r t -> p (r t)")
+            )
+            nc.sync.dma_start(out_words[:, loans], risk_codes[:])
+
+        before = None
+        for c in range(len(CHUNKS)):
+            risk = risks(c)
+            if c > 0:
+                planes(c - 1, before)
+            before = risk
+        planes(len(CHUNKS) - 1, before)
+
+        for q in range(4):
+            nc.sync.dma_start(
+                out_2[0, 4 * q : 4 * q + 4, :].bitcast(I32), out_scales[32 * q : 32 * q + 4, :].bitcast(I32)
+            )

@@ -19,7 +19,8 @@ COPY = mybir.ActivationFunctionType.Copy
 P = 128
 PACK = 4
 HALF = N // 2
-CHUNKS = (256, 256, 256, 128, 128)
+CHUNKS = (128, 256, 256, 256, 128)
+SCALAR_SHARE = (0, 0, 0, 1, 4)
 LANES = 16
 RUN = 4
 
@@ -59,8 +60,8 @@ def tile_picked_yborrow_max_po_kernel(
                 halves.append(tile)
             return halves
 
-        def pick(table, offsets, dtype, name):
-            picked = keep.tile([P, S], dtype, name=name, align_bytes=64)
+        def pick(table, offsets, dtype, name, tag):
+            picked = keep.tile([P, S], dtype, name=name, tag=tag, align_bytes=64)
             nc.vector.tensor_copy(picked[:], table[:].bitcast(dtype).indirect(offsets[:]))
             return picked
 
@@ -70,8 +71,8 @@ def tile_picked_yborrow_max_po_kernel(
         def on_scalar(out, in_):
             nc.scalar.activation(out, in_, COPY)
 
-        def quantise_weight(halves, casts, name, codes_tag):
-            rounded = keep.tile([P, PACK, P, PACK], BF16, name=f"{name}_bf", tag="weight_rounded", align_bytes=64)
+        def quantise_weight(halves, casts, name, codes_tag, rounded_tag):
+            rounded = keep.tile([P, PACK, P, PACK], BF16, name=f"{name}_bf", tag=rounded_tag, align_bytes=64)
             for h in range(2):
                 cols = slice(h * P // 2, (h + 1) * P // 2)
                 casts[h](
@@ -99,13 +100,13 @@ def tile_picked_yborrow_max_po_kernel(
                 stop=True,
             )
 
-        def first_layer(weight, codes, scales, name):
+        def first_layer(weight, codes, scales, name, leave):
             rows = []
             for t in range(PACK):
                 bank = psum.tile([P, S], F32, name="bank")
                 product(bank[:], weight, t, codes[:], scales[:])
                 row = keep.tile([P, S], F32, name=f"{name}{t}")
-                nc.scalar.copy(row[:], bank[:])
+                leave(row[:], bank[:])
                 rows.append(row)
             return rows
 
@@ -119,33 +120,33 @@ def tile_picked_yborrow_max_po_kernel(
         e_word_table = load_words(e_words, "e_word_table")
         e_scale_table = load_scales(e_scales, "e_scale_table", nc.vector)
         w2_raw = load_weight(w2, "w2")
-        w1_raw = load_weight(w1, "w1")
         x_scale_table = load_scales(x_scales, "x_scale_table", nc.gpsimd)
         x_word_table = load_words(x_words, "x_word_table")
+        w1_raw = load_weight(w1, "w1")
         w3_raw = load_weight(w3, "w3")
 
         starts = [sum(CHUNKS[:c]) for c in range(len(CHUNKS))]
 
-        def look_up(move, rows, offsets, c, tile):
+        def look_up(moves, rows, offsets, c, tile):
             entries = slice(starts[c] // LANES, (starts[c] + CHUNKS[c]) // LANES)
             for t in range(PACK):
-                move(tile[:, t, :], rows[t][:].indirect(offsets[:, entries]))
+                moves[t](tile[:, t, :], rows[t][:].indirect(offsets[:, entries]))
             return tile
 
         def lender_tile(c):
-            return keep.tile([P, PACK, CHUNKS[c]], F32, name=f"lender{c}", tag=f"lender_slot{c % 2}", align_bytes=64)
+            return keep.tile([P, PACK, CHUNKS[c]], F32, name=f"lender{c}", tag=f"lender_slot{c % 3}", align_bytes=64)
 
-        e_picked_words = pick(e_word_table, ldr_sb, U32, "e_picked_words")
-        e_picked_scales = pick(e_scale_table, ldr_sb, U8, "e_picked_scales")
-        w2_mx = quantise_weight(w2_raw, (on_scalar, on_vector), "w2", "w2_codes")
-        ye = first_layer(w2_mx, e_picked_words, e_picked_scales, "ye")
-        first_lender = look_up(on_scalar, ye, ln_sb, 0, lender_tile(0))
+        e_picked_words = pick(e_word_table, ldr_sb, U32, "e_picked_words", "e_picked_words")
+        e_picked_scales = pick(e_scale_table, ldr_sb, U8, "e_picked_scales", "e_picked_scales")
+        w2_mx = quantise_weight(w2_raw, (on_scalar, on_vector), "w2", "w2_codes", "w2_rounded")
+        ye = first_layer(w2_mx, e_picked_words, e_picked_scales, "ye", nc.scalar.copy)
+        early_lenders = [look_up([on_scalar] * PACK, ye, ln_sb, c, lender_tile(c)) for c in range(2)]
 
-        w1_mx = quantise_weight(w1_raw, (on_vector, on_vector), "w1", "lender_slot1")
-        x_picked_scales = pick(x_scale_table, offs_sb, U8, "x_picked_scales")
-        x_picked_words = pick(x_word_table, offs_sb, U32, "x_picked_words")
-        y = first_layer(w1_mx, x_picked_words, x_picked_scales, "y")
-        w3_mx = quantise_weight(w3_raw, (on_vector, on_vector), "w3", "w3_codes")
+        x_picked_scales = pick(x_scale_table, offs_sb, U8, "x_picked_scales", "w2_rounded")
+        x_picked_words = pick(x_word_table, offs_sb, U32, "x_picked_words", "x_picked_words")
+        w1_mx = quantise_weight(w1_raw, (on_vector, on_vector), "w1", "lender_slot2", "w1_rounded")
+        y = first_layer(w1_mx, x_picked_words, x_picked_scales, "y", nc.vector.tensor_copy)
+        w3_mx = quantise_weight(w3_raw, (on_vector, on_vector), "w3", "w3_codes", "w1_rounded")
 
         y_unit = []
         for t in range(PACK):
@@ -165,15 +166,15 @@ def tile_picked_yborrow_max_po_kernel(
 
         def risks(c):
             width = CHUNKS[c]
-            borrower = look_up(on_scalar, y, bo_sb, c, ring.tile([P, PACK, width], F32, name="borrower"))
-            lender = first_lender if c == 0 else look_up(on_scalar, ye, ln_sb, c, lender_tile(c))
-            move = on_scalar if c == len(CHUNKS) - 1 else on_vector
-            guarantor = look_up(move, y_unit, gu_sb, c, ring.tile([P, PACK, width], F32, name="guarantor"))
+            borrower = look_up([on_scalar] * PACK, y, bo_sb, c, ring.tile([P, PACK, width], F32, name="borrower"))
+            lender = early_lenders[c] if c < 2 else look_up([on_scalar] * PACK, ye, ln_sb, c, lender_tile(c))
+            moves = [on_scalar if t < SCALAR_SHARE[c] else on_vector for t in range(PACK)]
+            guarantor = look_up(moves, y_unit, gu_sb, c, ring.tile([P, PACK, width], F32, name="guarantor"))
             larger = ring.tile([P, PACK, width], F32, name="larger")
             nc.vector.tensor_tensor(larger[:], borrower[:], lender[:], MAX)
-            hid = keep.tile([P, width, PACK], BF16, name=f"hid{c}", tag="rounded_slot", align_bytes=64)
+            hid = keep.tile([P, width, PACK], BF16, name=f"hid{c}", tag=f"rounded_slot{c}", align_bytes=64)
             nc.vector.tensor_tensor(interleaved(hid), by_runs(larger), by_runs(guarantor), MULT)
-            hid_codes = keep.tile([P, width], U32, name=f"hid_codes{c}", tag=f"lender_slot{c % 2}", align_bytes=64)
+            hid_codes = keep.tile([P, width], U32, name=f"hid_codes{c}", tag=f"lender_slot{c % 3}", align_bytes=64)
             hid_scales = ring.tile([P, width], U8, name="hid_scales", align_bytes=64)
             nc.vector.quantize_mx(hid_codes[:].bitcast(FP8X4), hid_scales[:], hid[:].rearrange("p r t -> p (r t)"))
             risk = ring.tile([P, PACK, width], F32, name="risk", bufs=3)
@@ -189,7 +190,7 @@ def tile_picked_yborrow_max_po_kernel(
         def planes(c, risk):
             width = CHUNKS[c]
             loans = slice(starts[c], starts[c] + width)
-            risk_bf = keep.tile([P, width, PACK], BF16, name=f"risk_bf{c}", tag="rounded_slot", align_bytes=64)
+            risk_bf = keep.tile([P, width, PACK], BF16, name=f"risk_bf{c}", tag=f"rounded_slot{c + 1}", align_bytes=64)
             nc.vector.tensor_copy(interleaved(risk_bf), by_runs(risk))
             risk_codes = ring.tile([P, width], I32, name="risk_codes", align_bytes=64)
             nc.vector.quantize_mx(
@@ -206,6 +207,6 @@ def tile_picked_yborrow_max_po_kernel(
         planes(len(CHUNKS) - 1, before)
 
         for q in range(4):
-            nc.sync.dma_start(
+            (nc.sync, nc.scalar)[q % 2].dma_start(
                 out_2[0, 4 * q : 4 * q + 4, :].bitcast(I32), out_scales[32 * q : 32 * q + 4, :].bitcast(I32)
             )

@@ -13,6 +13,7 @@ U16 = mybir.dt.uint16
 U8 = mybir.dt.uint8
 FP8X4 = mybir.dt.float8_e4m3fn_x4
 MULT = mybir.AluOpType.mult
+ADD = mybir.AluOpType.add
 MAX = mybir.AluOpType.max
 COPY = mybir.ActivationFunctionType.Copy
 
@@ -151,7 +152,7 @@ def tile_picked_yborrow_max_po_kernel(
         y_unit = []
         for t in range(PACK):
             row = keep.tile([P, S], F32, name=f"y_unit{t}")
-            nc.vector.tensor_scalar(row[:], y[t][:], unit_sb[:, t : t + 1], None, MULT)
+            nc.gpsimd.tensor_scalar(row[:], y[t][:], unit_sb[:, t : t + 1], 0.0, MULT, ADD)
             y_unit.append(row)
 
         out_rows = out_0.rearrange("(p t) r -> p t r", t=PACK)

from contextlib import ExitStack

import concourse.mybir as mybir

K, T, S, N, H, W, U = 512, 2048, 512, 512, 512, 1024, 1024
FLOPS = 2 * K * N * S * 2 + 2 * H * N * U

F32 = mybir.dt.float32
BF16 = mybir.dt.bfloat16
I32 = mybir.dt.int32
U32 = mybir.dt.uint32
U16 = mybir.dt.uint16
U8 = mybir.dt.uint8
FP8X4 = mybir.dt.float8_e4m3fn_x4
MULT = mybir.AluOpType.mult
ADD = mybir.AluOpType.add
MAX = mybir.AluOpType.max
COPY = mybir.ActivationFunctionType.Copy

P = 128
PACK = 4
HALF = N // 2
CHUNKS = (128, 256, 256, 256, 128)
SCALAR_SHARE = (0, 0, 0, 1, 4)
LANES = 16
RUN = 4


def tile_picked_yborrow_max_po_kernel(
    tc, x_words, x_scales, w1, e_words, e_scales, w2, unit, w3, offs, ldr, bo, ln, gu, out_0, out_1, out_2
):
    nc = tc.nc
    with ExitStack() as ctx:
        keep = ctx.enter_context(tc.tile_pool(name="keep", bufs=1))
        ring = ctx.enter_context(tc.tile_pool(name="ring", bufs=2))
        psum = ctx.enter_context(tc.psum_pool(name="psum", bufs=8))

        def load_list(src, name):
            tile = keep.tile(list(src.shape), U16, name=name)
            nc.sync.dma_start(tile[:], src)
            return tile

        def load_scales(src, name, clear):
            tile = keep.tile([P, src.shape[2]], U8, name=name, align_bytes=64)
            clear.memset(tile[:].bitcast(I32), 0)
            for q in range(4):
                nc.sync.dma_start(tile[32 * q : 32 * q + 4, :].bitcast(I32), src[0, 4 * q : 4 * q + 4, :].bitcast(I32))
            return tile

        def load_words(src, name):
            tile = keep.tile([P, src.shape[2]], I32, name=name, align_bytes=64)
            nc.sync.dma_start(tile[:], src[0].rearrange("p n t -> p (n t)").bitcast(I32))
            return tile

        def load_weight(src, name):
            rows = src.rearrange("(p j) c -> p j c", j=PACK)
            halves = []
            for h in range(2):
                tile = keep.tile([P, PACK, HALF], F32, name=f"{name}_raw{h}")
                nc.sync.dma_start(tile[:], rows[:, :, h * HALF : (h + 1) * HALF])
                halves.append(tile)
            return halves

        def pick(table, offsets, dtype, name, tag):
            picked = keep.tile([P, S], dtype, name=name, tag=tag, align_bytes=64)
            nc.vector.tensor_copy(picked[:], table[:].bitcast(dtype).indirect(offsets[:]))
            return picked

        def on_vector(out, in_):
            nc.vector.tensor_copy(out, in_)

        def on_scalar(out, in_):
            nc.scalar.activation(out, in_, COPY)

        def quantise_weight(halves, casts, name, codes_tag, rounded_tag):
            rounded = keep.tile([P, PACK, P, PACK], BF16, name=f"{name}_bf", tag=rounded_tag, align_bytes=64)
            for h in range(2):
                cols = slice(h * P // 2, (h + 1) * P // 2)
                casts[h](
                    rounded[:, :, cols, :].rearrange("p t m j -> p m j t"),
                    halves[h][:].rearrange("p j (m t) -> p m j t", t=PACK),
                )
            codes = keep.tile([P, N], U32, name=f"{name}_codes", tag=codes_tag, align_bytes=64)
            scales = keep.tile([P, N], U8, name=f"{name}_scales", align_bytes=64)
            for t in range(PACK):
                cols = slice(t * P, (t + 1) * P)
                nc.vector.quantize_mx(
                    codes[:, cols].bitcast(FP8X4), scales[:, cols], rounded[:, t].rearrange("p m j -> p (m j)")
                )
            return codes, scales

        def product(out, weight, t, codes, scales):
            cols = slice(t * P, (t + 1) * P)
            nc.tensor.matmul_mx(
                out,
                lhsT=weight[0][:, cols].bitcast(FP8X4),
                lhsT_scale=weight[1][:, cols],
                rhs=codes.bitcast(FP8X4),
                rhs_scale=scales,
                start=True,
                stop=True,
            )

        def first_layer(weight, codes, scales, name, leave):
            rows = []
            for t in range(PACK):
                bank = psum.tile([P, S], F32, name="bank")
                product(bank[:], weight, t, codes[:], scales[:])
                row = keep.tile([P, S], F32, name=f"{name}{t}")
                leave(row[:], bank[:])
                rows.append(row)
            return rows

        ldr_sb = load_list(ldr, "ldr_sb")
        offs_sb = load_list(offs, "offs_sb")
        ln_sb = load_list(ln, "ln_sb")
        bo_sb = load_list(bo, "bo_sb")
        gu_sb = load_list(gu, "gu_sb")
        unit_sb = keep.tile([P, PACK], F32, name="unit_sb")
        nc.sync.dma_start(unit_sb[:], unit.rearrange("(p t) o -> p (t o)", t=PACK))
        e_word_table = load_words(e_words, "e_word_table")
        e_scale_table = load_scales(e_scales, "e_scale_table", nc.vector)
        w2_raw = load_weight(w2, "w2")
        x_scale_table = load_scales(x_scales, "x_scale_table", nc.gpsimd)
        x_word_table = load_words(x_words, "x_word_table")
        w1_raw = load_weight(w1, "w1")
        w3_raw = load_weight(w3, "w3")

        starts = [sum(CHUNKS[:c]) for c in range(len(CHUNKS))]

        def look_up(moves, rows, offsets, c, tile):
            entries = slice(starts[c] // LANES, (starts[c] + CHUNKS[c]) // LANES)
            for t in range(PACK):
                moves[t](tile[:, t, :], rows[t][:].indirect(offsets[:, entries]))
            return tile

        def lender_tile(c):
            return keep.tile([P, PACK, CHUNKS[c]], F32, name=f"lender{c}", tag=f"lender_slot{c % 3}", align_bytes=64)

        e_picked_words = pick(e_word_table, ldr_sb, U32, "e_picked_words", "e_picked_words")
        e_picked_scales = pick(e_scale_table, ldr_sb, U8, "e_picked_scales", "e_picked_scales")
        w2_mx = quantise_weight(w2_raw, (on_scalar, on_vector), "w2", "w2_codes", "w2_rounded")
        ye = first_layer(w2_mx, e_picked_words, e_picked_scales, "ye", nc.scalar.copy)
        early_lenders = [look_up([on_scalar] * PACK, ye, ln_sb, c, lender_tile(c)) for c in range(2)]

        x_picked_scales = pick(x_scale_table, offs_sb, U8, "x_picked_scales", "w2_rounded")
        x_picked_words = pick(x_word_table, offs_sb, U32, "x_picked_words", "x_picked_words")
        w1_mx = quantise_weight(w1_raw, (on_vector, on_vector), "w1", "lender_slot2", "w1_rounded")
        y = first_layer(w1_mx, x_picked_words, x_picked_scales, "y", nc.vector.tensor_copy)
        w3_mx = quantise_weight(w3_raw, (on_vector, on_vector), "w3", "w3_codes", "w1_rounded")

        y_unit = []
        for t in range(PACK):
            row = keep.tile([P, S], F32, name=f"y_unit{t}")
            nc.gpsimd.tensor_scalar(row[:], y[t][:], unit_sb[:, t : t + 1], 0.0, MULT, ADD)
            y_unit.append(row)

        out_rows = out_0.rearrange("(p t) r -> p t r", t=PACK)
        out_words = out_1[0].rearrange("p c t -> p (c t)").bitcast(I32)
        out_scales = keep.tile([P, U], U8, name="out_scales", align_bytes=64)

        def interleaved(tile):
            return tile[:].rearrange("p (c i) t -> p c t i", i=RUN)

        def by_runs(tile):
            return tile[:].rearrange("p t (c i) -> p c t i", i=RUN)

        def risks(c):
            width = CHUNKS[c]
            borrower = look_up([on_scalar] * PACK, y, bo_sb, c, ring.tile([P, PACK, width], F32, name="borrower"))
            lender = early_lenders[c] if c < 2 else look_up([on_scalar] * PACK, ye, ln_sb, c, lender_tile(c))
            moves = [on_scalar if t < SCALAR_SHARE[c] else on_vector for t in range(PACK)]
            guarantor = look_up(moves, y_unit, gu_sb, c, ring.tile([P, PACK, width], F32, name="guarantor"))
            larger = ring.tile([P, PACK, width], F32, name="larger")
            nc.vector.tensor_tensor(larger[:], borrower[:], lender[:], MAX)
            hid = keep.tile([P, width, PACK], BF16, name=f"hid{c}", tag=f"rounded_slot{c}", align_bytes=64)
            nc.vector.tensor_tensor(interleaved(hid), by_runs(larger), by_runs(guarantor), MULT)
            hid_codes = keep.tile([P, width], U32, name=f"hid_codes{c}", tag=f"lender_slot{c % 3}", align_bytes=64)
            hid_scales = ring.tile([P, width], U8, name="hid_scales", align_bytes=64)
            nc.vector.quantize_mx(hid_codes[:].bitcast(FP8X4), hid_scales[:], hid[:].rearrange("p r t -> p (r t)"))
            risk = ring.tile([P, PACK, width], F32, name="risk", bufs=3)
            per_bank = S // width
            for t0 in range(0, PACK, per_bank):
                bank = psum.tile([P, per_bank, width], F32, name="bank")
                for u in range(per_bank):
                    product(bank[:, u, :], w3_mx, t0 + u, hid_codes[:], hid_scales[:])
                nc.scalar.copy(risk[:, t0 : t0 + per_bank, :], bank[:])
            nc.sync.dma_start(out_rows[:, :, starts[c] : starts[c] + width], risk[:])
            return risk

        def planes(c, risk):
            width = CHUNKS[c]
            loans = slice(starts[c], starts[c] + width)
            risk_bf = keep.tile([P, width, PACK], BF16, name=f"risk_bf{c}", tag=f"rounded_slot{c + 1}", align_bytes=64)
            nc.vector.tensor_copy(interleaved(risk_bf), by_runs(risk))
            risk_codes = ring.tile([P, width], I32, name="risk_codes", align_bytes=64)
            nc.vector.quantize_mx(
                risk_codes[:].bitcast(FP8X4), out_scales[:, loans], risk_bf[:].rearrange("p r t -> p (r t)")
            )
            nc.sync.dma_start(out_words[:, loans], risk_codes[:])

        before = None
        for c in range(len(CHUNKS)):
            risk = risks(c)
            if c > 0:
                planes(c - 1, before)
            before = risk
        planes(len(CHUNKS) - 1, before)

        for q in range(4):
            (nc.sync, nc.scalar)[q % 2].dma_start(
                out_2[0, 4 * q : 4 * q + 4, :].bitcast(I32), out_scales[32 * q : 32 * q + 4, :].bitcast(I32)
            )
